import numpy as np
import ml_dtypes


def mxq(x, axis, fmt="e4m3"):
    dtype, down = {"e4m3": (ml_dtypes.float8_e4m3fn, 7), "e5m2": (ml_dtypes.float8_e5m2, 14)}[fmt]
    v = np.moveaxis(np.asarray(x, np.float32).astype(ml_dtypes.bfloat16).astype(np.float64), axis, -1)
    blocks = v.reshape(v.shape[:-1] + (-1, 32))
    amax = np.abs(blocks).max(-1, keepdims=True)
    byte = np.maximum(np.where(amax > 0, np.frexp(amax)[1] - 1 + 127, 0) - down, 1)
    scale = np.exp2(byte - 127.0)
    codes = (blocks / scale).astype(np.float32).astype(dtype).astype(np.float64)
    return np.moveaxis((codes * scale).reshape(v.shape), -1, axis)


WIDE = False


def mx_kscale(k):
    if not WIDE:
        return np.ones(k)
    levels = np.array([10, -10, 5, -5, 0])
    if k % 512:
        return np.exp2(np.random.permutation(np.resize(levels, k // 32))).repeat(32)
    a = np.empty((k // 512, 16))
    for p in range(k // 512):
        a[p, :8] = np.random.permutation(np.resize(levels, 8))
        for g in range(8):
            far = levels[np.abs(levels - a[p, g]) >= 10]
            a[p, g + 8] = far[np.random.randint(len(far))]
    return np.exp2(a.ravel()).repeat(32)


def f64(x):
    return np.asarray(x).astype(np.float64)


def striped(idx):
    return np.tile(np.asarray(idx).reshape(-1, 16).T, (8, 1)).astype(np.uint16)


def unstriped(offs):
    return offs[:16].T.reshape(-1).astype(np.int64)


def striped8(idx):
    return np.asarray(idx).reshape(8, -1, 16).transpose(0, 2, 1).reshape(128, -1).astype(np.uint16)


def unstriped8(offs):
    return offs.reshape(8, 16, -1).transpose(0, 2, 1).reshape(8, -1).astype(np.int64)


def pick8(x, idx, run):
    r = np.arange(len(x))
    return x[r[:, None], idx[r % (8 * run) // run]]


E2M1 = np.array([0.0, 0.5, 1.0, 1.5, 2.0, 3.0, 4.0, 6.0, -0.0, -0.5, -1.0, -1.5, -2.0, -3.0, -4.0, -6.0])


def pack_weight(w, fmt):
    k, n = w.shape
    w = f64(np.asarray(w, np.float32).astype(ml_dtypes.bfloat16)).reshape(k // 32, 32, n)
    amax = np.abs(w).max(1)
    if fmt == "e4m3":
        byte = np.frexp(amax)[1] - 1 + 127 - 7
    else:
        mant, ex = np.frexp(amax / 6.0)
        byte = np.where(mant > 0.5, ex, ex - 1) + 127
    byte = np.clip(np.where(amax > 0, byte, 1), 1, 254)
    scaled = (w * np.exp2(127.0 - byte)[:, None, :]).reshape(k, n).astype(np.float32)
    by_word = np.ascontiguousarray(scaled.reshape(k // 512, 128, 4, n).transpose(0, 1, 3, 2))
    if fmt == "e4m3":
        words = by_word.astype(ml_dtypes.float8_e4m3fn).view(np.uint8)
    else:
        c = by_word.astype(ml_dtypes.float4_e2m1fn).view(np.uint8) & 0xF
        words = (c[..., 0::2] | (c[..., 1::2] << 4)).reshape(k // 512, 128, 2 * n)
    return np.ascontiguousarray(words), np.ascontiguousarray(byte.astype(np.uint8).reshape(k // 512, 16, n))


def unpack_weight(words, scales, fmt):
    g, _, n = scales.shape
    words = np.ascontiguousarray(words).reshape(g, 128, n, -1)
    if fmt == "e4m3":
        vals = words.view(ml_dtypes.float8_e4m3fn).astype(np.float64)
    else:
        nib = np.empty((g, 128, n, 4), np.uint8)
        nib[..., 0::2] = words & 0xF
        nib[..., 1::2] = words >> 4
        vals = E2M1[nib]
    vals = vals * np.repeat(np.exp2(scales.astype(np.float64) - 127.0), 8, axis=1)[..., None]
    return vals.transpose(0, 1, 3, 2).reshape(g * 512, n)


K, R, F, T, J, U = 512, 128, 512, 2048, 512, 1024


def setup_inputs():
    n = np.random.standard_normal
    idx = np.random.permutation(T)[:J]
    idx2 = np.stack([np.random.permutation(U)[:J] for _ in range(8)])
    idx3 = np.stack([np.random.permutation(U)[:J] for _ in range(8)])
    fk = mx_kscale(K)
    ff = mx_kscale(F)
    tabp = pack_weight(n((K, T)) / fk[:, None], "e2m1")
    return {
        "tab_words": tabp[0],
        "tab_scales": tabp[1],
        "w1": (n((K, R)) * 1 / np.sqrt(K) * fk[:, None]).astype(np.float32),
        "gain": (np.random.uniform(0.5, 1.5, (R, 1))).astype(np.float32),
        "ground": (n((R, U)) * 0.7).astype(np.float32),
        "wo": (n((F, R)) * 1 / np.sqrt(F) * ff[:, None]).astype(np.float32),
        "dy": (n((F, U)) / ff[:, None]).astype(np.float32),
        "og": (np.random.uniform(0.3, 1.0, (R, 1))).astype(np.float32),
        "base": (0.3 * n((R, J))).astype(np.float32),
        "offs": striped(idx),
        "offs2": striped8(idx2),
        "offs3": striped8(idx3),
    }


def reference(tab_words, tab_scales, w1, gain, ground, wo, dy, og, base, offs, offs2, offs3):
    idx = unstriped(offs)
    idx2 = unstriped8(offs2)
    idx3 = unstriped8(offs3)
    tabu = unpack_weight(tab_words, tab_scales, "e2m1")
    w1q = mxq(f64(w1), 0, "e4m3")
    tabidxg = tabu[:, idx]
    a = w1q.T @ tabidxg
    h1 = a * f64(gain)
    pa = np.zeros((R, U))
    pa[np.arange(R)[:, None], idx2[np.arange(R) % 128 // 16]] = h1
    pb = np.zeros((R, U))
    pb[np.arange(R)[:, None], idx3[np.arange(R) % 128 // 16]] = a
    woq = mxq(f64(wo), 0, "e4m3")
    dyq = mxq(f64(dy), 0, "e4m3")
    c0 = woq.T @ dyq
    dpb = c0 * np.tanh(pa + f64(ground))
    dpa = c0 * (pb + f64(ground)) * (1.0 - np.square(np.tanh(pa + f64(ground))))
    dh1 = pick8(dpa, idx2, 16)
    da = pick8(dpb, idx3, 16) + dh1 * f64(gain)
    hda = da * 2.0
    hdh1 = hda * f64(gain)
    s51 = np.zeros((R, U))
    s51[np.arange(R)[:, None], idx2[np.arange(R) % 128 // 16]] = hdh1
    s52 = np.zeros((R, U))
    s52[np.arange(R)[:, None], idx3[np.arange(R) % 128 // 16]] = hda
    hpb = s51 * (1.0 - np.square(np.tanh(pa + f64(ground)))) * c0
    hpa = s51 * c0 * (pb + f64(ground)) * (-1.0) * np.tanh(pa + f64(ground)) * 2.0 * (1.0 - np.square(np.tanh(pa + f64(ground)))) + s52 * c0 * (1.0 - np.square(np.tanh(pa + f64(ground))))
    hh1 = pick8(hpa, idx2, 16)
    ha = pick8(hpb, idx3, 16) + hh1 * f64(gain)
    y = ha * f64(og) + f64(base)
    return y

@@ -1,0 +1,191 @@
+from contextlib import ExitStack
+
+import concourse.mybir as mybir
+
+K, R, F, T, J, U = 512, 128, 512, 2048, 512, 1024
+FLOPS = 2 * K * R * J + 2 * F * R * U
+
+F32 = mybir.dt.float32
+BF16 = mybir.dt.bfloat16
+I32 = mybir.dt.int32
+U32 = mybir.dt.uint32
+U16 = mybir.dt.uint16
+U8 = mybir.dt.uint8
+FP8X4 = mybir.dt.float8_e4m3fn_x4
+FP4X4 = mybir.dt.float4_e2m1fn_x4
+ALU = mybir.AluOpType
+ACT = mybir.ActivationFunctionType
+
+P = 128
+PACK = 4
+JH = J // 2
+UH = U // 2
+DY_CHUNK = 256
+
+
+def interleave(copy, grouped, raw):
+    copy(grouped.rearrange("p (c i) t -> p c t i", i=4), raw.rearrange("p t (c i) -> p c t i", i=4))
+
+
+def tile_attend_gptwopages_kernel(tc, tab_words, tab_scales, w1, gain, ground, wo, dy, og, base, offs, offs2, offs3, out):
+    nc = tc.nc
+    with ExitStack() as ctx:
+        sb = ctx.enter_context(tc.tile_pool(name="sb", bufs=1))
+        ps = ctx.enter_context(tc.psum_pool(name="ps", bufs=1))
+
+        def tile(name, shape, dtype):
+            return sb.tile(shape, dtype, name=name, align_bytes=64)
+
+        list1 = tile("list1", [P, J // 16], U16)
+        list2 = tile("list2", [P, J // 16], U16)
+        list3 = tile("list3", [P, J // 16], U16)
+        words = tile("words", [P, T], U16)
+        scales = tile("scales", [P, T], U8)
+        w1_raw = tile("w1_raw", [P, PACK, R], F32)
+        wo_raw = tile("wo_raw", [P, PACK, R], F32)
+        dy_raw = [tile(f"dy_raw{c}", [P, PACK, DY_CHUNK], F32) for c in range(U // DY_CHUNK)]
+        gain_col = tile("gain_col", [P, 1], F32)
+        og_col = tile("og_col", [P, 1], F32)
+        ground_sb = tile("ground_sb", [P, U], F32)
+        base_sb = tile("base_sb", [P, J], F32)
+        page2 = tile("page2", [P, U], F32)
+        page3 = tile("page3", [P, U], F32)
+        warm = tile("warm", [P, 8], F32)
+
+        nc.vector.memset(scales[:].bitcast(I32), 0)
+        nc.vector.memset(warm[:], 0.0)
+        nc.scalar.activation(warm[:], warm[:], ACT.Tanh)
+        nc.vector.memset(page2[:], 0.0)
+        nc.vector.memset(page3[:], 0.0)
+
+        nc.sync.dma_start(list1[:], offs)
+        nc.sync.dma_start(w1_raw[:], w1.rearrange("(p j) r -> p j r", j=PACK))
+        for q in range(4):
+            nc.sync.dma_start(scales[32 * q : 32 * q + 4, :].bitcast(I32), tab_scales[0, 4 * q : 4 * q + 4, :].bitcast(I32))
+        nc.sync.dma_start(words[:].bitcast(I32), tab_words[0].bitcast(I32))
+        nc.sync.dma_start(gain_col[:], gain)
+        nc.sync.dma_start(list2[:], offs2)
+        nc.sync.dma_start(wo_raw[:], wo.rearrange("(p j) r -> p j r", j=PACK))
+        dy_view = dy.rearrange("(p j) u -> p j u", j=PACK)
+        for c in range(U // DY_CHUNK):
+            nc.sync.dma_start(dy_raw[c][:], dy_view[:, :, c * DY_CHUNK : (c + 1) * DY_CHUNK])
+            if c == 1:
+                nc.sync.dma_start(ground_sb[:], ground)
+                nc.sync.dma_start(list3[:], offs3)
+        nc.sync.dma_start(og_col[:], og)
+        nc.sync.dma_start(base_sb[:], base)
+
+        def slots(lst, h):
+            return lst[:, h * (JH // 16) : (h + 1) * (JH // 16)]
+
+        def jh(h):
+            return slice(h * JH, (h + 1) * JH)
+
+        def uh(h):
+            return slice(h * UH, (h + 1) * UH)
+
+        w1_bf = tile("w1_bf", [P, R, PACK], BF16)
+        w1_codes = tile("w1_codes", [P, R], U32)
+        w1_scales = tile("w1_scales", [P, R], U8)
+        interleave(nc.vector.tensor_copy, w1_bf[:], w1_raw[:])
+        tab_scales_g = tile("tab_scales_g", [P, J], U8)
+        tab_words_g = tile("tab_words_g", [P, J], U16)
+        nc.vector.tensor_copy(tab_scales_g[:], scales[:].indirect(list1[:]))
+        nc.vector.quantize_mx(w1_codes[:].bitcast(FP8X4), w1_scales[:], w1_bf[:].rearrange("p r j -> p (r j)"))
+        a_sb = tile("a_sb", [P, J], F32)
+        h1 = tile("h1", [P, J], F32)
+        a_ps = [ps.tile([P, JH], F32, name=f"a_ps{h}") for h in range(2)]
+        for h in range(2):
+            nc.vector.tensor_copy(tab_words_g[:, jh(h)], words[:].indirect(slots(list1, h)))
+            nc.tensor.matmul_mx(a_ps[h][:], w1_codes[:].bitcast(FP8X4), w1_scales[:], tab_words_g[:, jh(h)].bitcast(FP4X4), tab_scales_g[:, jh(h)], start=True, stop=True)
+            nc.scalar.activation(h1[:, jh(h)], a_ps[h][:], ACT.Copy, scale=gain_col[:])
+        for h in range(2):
+            nc.scalar.copy(a_sb[:, jh(h)], a_ps[h][:])
+        for h in range(2):
+            nc.vector.tensor_copy(page2[:].indirect(slots(list2, h)), h1[:, jh(h)])
+        nc.vector.tensor_copy(page3[:].indirect(list3[:]), a_sb[:])
+
+        wo_bf = tile("wo_bf", [P, R, PACK], BF16)
+        wo_codes = tile("wo_codes", [P, R], U32)
+        wo_scales = tile("wo_scales", [P, R], U8)
+        interleave(nc.scalar.copy, wo_bf[:], wo_raw[:])
+        dy_bf = [tile(f"dy_bf{h}", [P, UH, PACK], BF16) for h in range(2)]
+        dy_codes = [tile(f"dy_codes{h}", [P, UH], U32) for h in range(2)]
+        dy_scales = [tile(f"dy_scales{h}", [P, UH], U8) for h in range(2)]
+        for c in range(U // DY_CHUNK):
+            h, part = divmod(c, UH // DY_CHUNK)
+            interleave(nc.scalar.copy, dy_bf[h][:, part * DY_CHUNK : (part + 1) * DY_CHUNK, :], dy_raw[c][:])
+        gain_row = tile("gain_row", [P, JH], F32)
+        nc.scalar.copy(gain_row[:], gain_col[:].to_broadcast([P, JH]))
+        gain2_col = tile("gain2_col", [P, 1], F32)
+        nc.scalar.mul(gain2_col[:], gain_col[:], 2.0)
+
+        x = tile("x", [P, U], F32)
+        t = tile("t", [P, U], F32)
+        t2 = tile("t2", [P, U], F32)
+        for h in range(2):
+            nc.vector.tensor_tensor(x[:, uh(h)], page2[:, uh(h)], ground_sb[:, uh(h)], ALU.add)
+            nc.scalar.activation(t[:, uh(h)], x[:, uh(h)], ACT.Tanh)
+        for h in range(2):
+            nc.scalar.activation(t2[:, uh(h)], t[:, uh(h)], ACT.Square)
+
+        nc.vector.quantize_mx(wo_codes[:].bitcast(FP8X4), wo_scales[:], wo_bf[:].rearrange("p r j -> p (r j)"))
+        c0 = [ps.tile([P, UH], F32, name=f"c0_{h}") for h in range(2)]
+        for h in range(2):
+            nc.vector.quantize_mx(dy_codes[h][:].bitcast(FP8X4), dy_scales[h][:], dy_bf[h][:].rearrange("p u j -> p (u j)"))
+            nc.tensor.matmul_mx(c0[h][:], wo_codes[:].bitcast(FP8X4), wo_scales[:], dy_codes[h][:].bitcast(FP8X4), dy_scales[h][:], start=True, stop=True)
+
+        b = tile("b", [P, U], F32)
+        dpa = tile("dpa", [P, U], F32)
+        dpb = tile("dpb", [P, U], F32)
+        ncs = tile("ncs", [P, U], F32)
+        for h in range(2):
+            nc.vector.tensor_tensor(b[:, uh(h)], page3[:, uh(h)], ground_sb[:, uh(h)], ALU.add)
+        for h in range(2):
+            nc.vector.tensor_tensor(dpb[:, uh(h)], c0[h][:], t[:, uh(h)], ALU.mult)
+        for h in range(2):
+            nc.vector.scalar_tensor_tensor(ncs[:, uh(h)], t2[:, uh(h)], 1.0, c0[h][:], ALU.subtract, ALU.mult)
+        for h in range(2):
+            nc.vector.scalar_tensor_tensor(dpa[:, uh(h)], ncs[:, uh(h)], -1.0, b[:, uh(h)], ALU.mult, ALU.mult)
+
+        dh1g = tile("dh1g", [P, J], F32)
+        da = tile("da", [P, J], F32)
+        hda = tile("hda", [P, J], F32)
+        hdh1 = tile("hdh1", [P, J], F32)
+        for h in range(2):
+            nc.vector.tensor_tensor(dh1g[:, jh(h)], dpa[:].indirect(slots(list2, h)), gain_row[:], ALU.mult)
+        for h in range(2):
+            nc.vector.tensor_tensor(da[:, jh(h)], dpb[:].indirect(slots(list3, h)), dh1g[:, jh(h)], ALU.add)
+            nc.scalar.activation(hdh1[:, jh(h)], da[:, jh(h)], ACT.Copy, scale=gain2_col[:])
+        nc.scalar.mul(hda[:], da[:], 2.0)
+        for h in range(2):
+            nc.vector.tensor_copy(page2[:].indirect(slots(list2, h)), hdh1[:, jh(h)])
+        nc.vector.tensor_copy(page3[:].indirect(list3[:]), hda[:])
+
+        cs = tile("cs", [P, U], F32)
+        tm2 = tile("tm2", [P, U], F32)
+        e = tile("e", [P, U], F32)
+        nc.scalar.mul(tm2[:], t[:], -2.0)
+        nc.scalar.mul(cs[:], ncs[:], -1.0)
+        nc.vector.tensor_tensor(e[:], tm2[:], dpa[:], ALU.mult)
+        hpa = tile("hpa", [P, U], F32)
+        hpb = tile("hpb", [P, U], F32)
+        m1 = tile("m1", [P, U], F32)
+        m2 = tile("m2", [P, U], F32)
+        nc.vector.tensor_tensor(m1[:], page2[:], e[:], ALU.mult)
+        for h in range(2):
+            nc.vector.tensor_tensor(m2[:, uh(h)], page3[:, uh(h)], cs[:, uh(h)], ALU.mult)
+        nc.vector.tensor_tensor(hpb[:], page2[:], cs[:], ALU.mult)
+        for h in range(2):
+            nc.vector.tensor_tensor(hpa[:, uh(h)], m1[:, uh(h)], m2[:, uh(h)], ALU.add)
+
+        hh1g = tile("hh1g", [P, J], F32)
+        ha = tile("ha", [P, J], F32)
+        y = tile("y", [P, J], F32)
+        for h in range(2):
+            nc.vector.tensor_tensor(hh1g[:, jh(h)], hpa[:].indirect(slots(list2, h)), gain_row[:], ALU.mult)
+        for h in range(2):
+            nc.vector.tensor_tensor(ha[:, jh(h)], hpb[:].indirect(slots(list3, h)), hh1g[:, jh(h)], ALU.add)
+        for h in range(2):
+            nc.vector.scalar_tensor_tensor(y[:, jh(h)], ha[:, jh(h)], og_col[:], base_sb[:, jh(h)], ALU.mult, ALU.add)
+            nc.sync.dma_start(out[:, jh(h)], y[:, jh(h)])

@@ -21,6 +21,9 @@ PACK = 4
 JH = J // 2
 UH = U // 2
 DY_CHUNK = 256
+DY_LOADS = (512, 256, 256)
+B_SPLIT = 768
+HPB_SPLIT = 384
 
 
 def interleave(copy, grouped, raw):
@@ -33,8 +36,8 @@ def tile_attend_gptwopages_kernel(tc, tab_words, tab_scales, w1, gain, ground, w
         sb = ctx.enter_context(tc.tile_pool(name="sb", bufs=1))
         ps = ctx.enter_context(tc.psum_pool(name="ps", bufs=1))
 
-        def tile(name, shape, dtype):
-            return sb.tile(shape, dtype, name=name, align_bytes=64)
+        def tile(name, shape, dtype, tag=None):
+            return sb.tile(shape, dtype, name=name, tag=tag or name, align_bytes=64)
 
         list1 = tile("list1", [P, J // 16], U16)
         list2 = tile("list2", [P, J // 16], U16)
@@ -43,7 +46,7 @@ def tile_attend_gptwopages_kernel(tc, tab_words, tab_scales, w1, gain, ground, w
         scales = tile("scales", [P, T], U8)
         w1_raw = tile("w1_raw", [P, PACK, R], F32)
         wo_raw = tile("wo_raw", [P, PACK, R], F32)
-        dy_raw = [tile(f"dy_raw{c}", [P, PACK, DY_CHUNK], F32) for c in range(U // DY_CHUNK)]
+        dy_raw = [tile(f"dy_raw{c}", [P, PACK, w], F32) for c, w in enumerate(DY_LOADS)]
         gain_col = tile("gain_col", [P, 1], F32)
         og_col = tile("og_col", [P, 1], F32)
         ground_sb = tile("ground_sb", [P, U], F32)
@@ -63,16 +66,16 @@ def tile_attend_gptwopages_kernel(tc, tab_words, tab_scales, w1, gain, ground, w
         for q in range(4):
             nc.sync.dma_start(scales[32 * q : 32 * q + 4, :].bitcast(I32), tab_scales[0, 4 * q : 4 * q + 4, :].bitcast(I32))
         nc.sync.dma_start(words[:].bitcast(I32), tab_words[0].bitcast(I32))
-        nc.sync.dma_start(gain_col[:], gain)
+        nc.gpsimd.dma_start(gain_col[:], gain)
+        nc.gpsimd.dma_start(og_col[:], og)
         nc.sync.dma_start(list2[:], offs2)
         nc.sync.dma_start(wo_raw[:], wo.rearrange("(p j) r -> p j r", j=PACK))
         dy_view = dy.rearrange("(p j) u -> p j u", j=PACK)
-        for c in range(U // DY_CHUNK):
-            nc.sync.dma_start(dy_raw[c][:], dy_view[:, :, c * DY_CHUNK : (c + 1) * DY_CHUNK])
-            if c == 1:
-                nc.sync.dma_start(ground_sb[:], ground)
-                nc.sync.dma_start(list3[:], offs3)
-        nc.sync.dma_start(og_col[:], og)
+        nc.sync.dma_start(dy_raw[0][:], dy_view[:, :, 0:512])
+        nc.sync.dma_start(list3[:], offs3)
+        nc.sync.dma_start(ground_sb[:], ground)
+        nc.sync.dma_start(dy_raw[1][:], dy_view[:, :, 512:768])
+        nc.sync.dma_start(dy_raw[2][:], dy_view[:, :, 768:1024])
         nc.sync.dma_start(base_sb[:], base)
 
         def slots(lst, h):
@@ -112,19 +115,20 @@ def tile_attend_gptwopages_kernel(tc, tab_words, tab_scales, w1, gain, ground, w
         dy_bf = [tile(f"dy_bf{h}", [P, UH, PACK], BF16) for h in range(2)]
         dy_codes = [tile(f"dy_codes{h}", [P, UH], U32) for h in range(2)]
         dy_scales = [tile(f"dy_scales{h}", [P, UH], U8) for h in range(2)]
+        dy_pieces = [dy_raw[0][:, :, :DY_CHUNK], dy_raw[0][:, :, DY_CHUNK:], dy_raw[1][:], dy_raw[2][:]]
         for c in range(U // DY_CHUNK):
             h, part = divmod(c, UH // DY_CHUNK)
-            interleave(nc.scalar.copy, dy_bf[h][:, part * DY_CHUNK : (part + 1) * DY_CHUNK, :], dy_raw[c][:])
+            interleave(nc.scalar.copy, dy_bf[h][:, part * DY_CHUNK : (part + 1) * DY_CHUNK, :], dy_pieces[c])
         gain_row = tile("gain_row", [P, JH], F32)
         nc.scalar.copy(gain_row[:], gain_col[:].to_broadcast([P, JH]))
         gain2_col = tile("gain2_col", [P, 1], F32)
         nc.scalar.mul(gain2_col[:], gain_col[:], 2.0)
 
         x = tile("x", [P, U], F32)
-        t = tile("t", [P, U], F32)
+        t = tile("t", [P, U], F32, tag="dy_raw2")
         t2 = tile("t2", [P, U], F32)
         for h in range(2):
-            nc.vector.tensor_tensor(x[:, uh(h)], page2[:, uh(h)], ground_sb[:, uh(h)], ALU.add)
+            nc.gpsimd.tensor_tensor(x[:, uh(h)], page2[:, uh(h)], ground_sb[:, uh(h)], ALU.add)
             nc.scalar.activation(t[:, uh(h)], x[:, uh(h)], ACT.Tanh)
         for h in range(2):
             nc.scalar.activation(t2[:, uh(h)], t[:, uh(h)], ACT.Square)
@@ -135,12 +139,12 @@ def tile_attend_gptwopages_kernel(tc, tab_words, tab_scales, w1, gain, ground, w
             nc.vector.quantize_mx(dy_codes[h][:].bitcast(FP8X4), dy_scales[h][:], dy_bf[h][:].rearrange("p u j -> p (u j)"))
             nc.tensor.matmul_mx(c0[h][:], wo_codes[:].bitcast(FP8X4), wo_scales[:], dy_codes[h][:].bitcast(FP8X4), dy_scales[h][:], start=True, stop=True)
 
-        b = tile("b", [P, U], F32)
+        b = tile("b", [P, U], F32, tag="dy_bf1")
         dpa = tile("dpa", [P, U], F32)
         dpb = tile("dpb", [P, U], F32)
         ncs = tile("ncs", [P, U], F32)
-        for h in range(2):
-            nc.vector.tensor_tensor(b[:, uh(h)], page3[:, uh(h)], ground_sb[:, uh(h)], ALU.add)
+        nc.gpsimd.tensor_tensor(b[:, :B_SPLIT], page3[:, :B_SPLIT], ground_sb[:, :B_SPLIT], ALU.add)
+        nc.vector.tensor_tensor(b[:, B_SPLIT:], page3[:, B_SPLIT:], ground_sb[:, B_SPLIT:], ALU.add)
         for h in range(2):
             nc.vector.tensor_tensor(dpb[:, uh(h)], c0[h][:], t[:, uh(h)], ALU.mult)
         for h in range(2):
@@ -164,18 +168,19 @@ def tile_attend_gptwopages_kernel(tc, tab_words, tab_scales, w1, gain, ground, w
 
         cs = tile("cs", [P, U], F32)
         tm2 = tile("tm2", [P, U], F32)
-        e = tile("e", [P, U], F32)
+        e = tile("e", [P, U], F32, tag="dpb")
         nc.scalar.mul(tm2[:], t[:], -2.0)
         nc.scalar.mul(cs[:], ncs[:], -1.0)
-        nc.vector.tensor_tensor(e[:], tm2[:], dpa[:], ALU.mult)
+        nc.gpsimd.tensor_tensor(e[:], tm2[:], dpa[:], ALU.mult)
         hpa = tile("hpa", [P, U], F32)
         hpb = tile("hpb", [P, U], F32)
         m1 = tile("m1", [P, U], F32)
         m2 = tile("m2", [P, U], F32)
-        nc.vector.tensor_tensor(m1[:], page2[:], e[:], ALU.mult)
+        nc.gpsimd.tensor_tensor(m1[:], page2[:], e[:], ALU.mult)
+        nc.gpsimd.tensor_tensor(hpb[:, :HPB_SPLIT], page2[:, :HPB_SPLIT], cs[:, :HPB_SPLIT], ALU.mult)
         for h in range(2):
             nc.vector.tensor_tensor(m2[:, uh(h)], page3[:, uh(h)], cs[:, uh(h)], ALU.mult)
-        nc.vector.tensor_tensor(hpb[:], page2[:], cs[:], ALU.mult)
+        nc.vector.tensor_tensor(hpb[:, HPB_SPLIT:], page2[:, HPB_SPLIT:], cs[:, HPB_SPLIT:], ALU.mult)
         for h in range(2):
             nc.vector.tensor_tensor(hpa[:, uh(h)], m1[:, uh(h)], m2[:, uh(h)], ALU.add)
 

@@ -1,6 +1,7 @@
 from contextlib import ExitStack
 
 import concourse.mybir as mybir
+from concourse.masks import make_identity
 
 K, R, F, T, J, U = 512, 128, 512, 2048, 512, 1024
 FLOPS = 2 * K * R * J + 2 * F * R * U
@@ -22,8 +23,6 @@ JH = J // 2
 UH = U // 2
 DY_CHUNK = 256
 DY_LOADS = (512, 256, 256)
-B_SPLIT = 768
-HPB_SPLIT = 384
 
 
 def interleave(copy, grouped, raw):
@@ -55,7 +54,8 @@ def tile_attend_gptwopages_kernel(tc, tab_words, tab_scales, w1, gain, ground, w
         page3 = tile("page3", [P, U], F32)
         warm = tile("warm", [P, 8], F32)
 
-        nc.vector.memset(scales[:].bitcast(I32), 0)
+        nc.vector.memset(scales[:, : T // 2].bitcast(I32), 0)
+        nc.gpsimd.memset(scales[:, T // 2 :].bitcast(I32), 0)
         nc.vector.memset(warm[:], 0.0)
         nc.scalar.activation(warm[:], warm[:], ACT.Tanh)
         nc.vector.memset(page2[:], 0.0)
@@ -67,15 +67,15 @@ def tile_attend_gptwopages_kernel(tc, tab_words, tab_scales, w1, gain, ground, w
             nc.sync.dma_start(scales[32 * q : 32 * q + 4, :].bitcast(I32), tab_scales[0, 4 * q : 4 * q + 4, :].bitcast(I32))
         nc.sync.dma_start(words[:].bitcast(I32), tab_words[0].bitcast(I32))
         nc.gpsimd.dma_start(gain_col[:], gain)
-        nc.gpsimd.dma_start(og_col[:], og)
         nc.sync.dma_start(list2[:], offs2)
         nc.sync.dma_start(wo_raw[:], wo.rearrange("(p j) r -> p j r", j=PACK))
+        nc.sync.dma_start(list3[:], offs3)
         dy_view = dy.rearrange("(p j) u -> p j u", j=PACK)
         nc.sync.dma_start(dy_raw[0][:], dy_view[:, :, 0:512])
-        nc.sync.dma_start(list3[:], offs3)
         nc.sync.dma_start(ground_sb[:], ground)
         nc.sync.dma_start(dy_raw[1][:], dy_view[:, :, 512:768])
         nc.sync.dma_start(dy_raw[2][:], dy_view[:, :, 768:1024])
+        nc.sync.dma_start(og_col[:], og)
         nc.sync.dma_start(base_sb[:], base)
 
         def slots(lst, h):
@@ -87,102 +87,114 @@ def tile_attend_gptwopages_kernel(tc, tab_words, tab_scales, w1, gain, ground, w
         def uh(h):
             return slice(h * UH, (h + 1) * UH)
 
+        ident = tile("ident", [P, P], F32)
+        make_identity(nc, ident[:])
+
+        def turn_into(bank, src, first, last):
+            blocks = src.shape[1] // P
+            for j in range(blocks):
+                cols = slice(j * P, (j + 1) * P)
+                nc.tensor.matmul(bank[:, cols], src[:, cols], ident[:], start=first and j == 0, stop=last and j == blocks - 1, is_transpose=True)
+
+        gain_row = tile("gain_row", [P, JH], F32)
+        gain2_row = tile("gain2_row", [P, JH], F32)
+        nc.scalar.copy(gain_row[:], gain_col[:].to_broadcast([P, JH]))
+        nc.scalar.mul(gain2_row[:], gain_row[:], 2.0)
+
         w1_bf = tile("w1_bf", [P, R, PACK], BF16)
         w1_codes = tile("w1_codes", [P, R], U32)
         w1_scales = tile("w1_scales", [P, R], U8)
         interleave(nc.vector.tensor_copy, w1_bf[:], w1_raw[:])
         tab_scales_g = tile("tab_scales_g", [P, J], U8)
         tab_words_g = tile("tab_words_g", [P, J], U16)
-        nc.vector.tensor_copy(tab_scales_g[:], scales[:].indirect(list1[:]))
         nc.vector.quantize_mx(w1_codes[:].bitcast(FP8X4), w1_scales[:], w1_bf[:].rearrange("p r j -> p (r j)"))
         a_sb = tile("a_sb", [P, J], F32)
-        h1 = tile("h1", [P, J], F32)
-        a_ps = [ps.tile([P, JH], F32, name=f"a_ps{h}") for h in range(2)]
+        a_banks = ps.tile([P, 2, UH], F32, name="a_banks", tag="A")
+        a_ps = [a_banks[:, h, :JH] for h in range(2)]
         for h in range(2):
+            nc.vector.tensor_copy(tab_scales_g[:, jh(h)], scales[:].indirect(slots(list1, h)))
             nc.vector.tensor_copy(tab_words_g[:, jh(h)], words[:].indirect(slots(list1, h)))
-            nc.tensor.matmul_mx(a_ps[h][:], w1_codes[:].bitcast(FP8X4), w1_scales[:], tab_words_g[:, jh(h)].bitcast(FP4X4), tab_scales_g[:, jh(h)], start=True, stop=True)
-            nc.scalar.activation(h1[:, jh(h)], a_ps[h][:], ACT.Copy, scale=gain_col[:])
+            nc.tensor.matmul_mx(a_ps[h], w1_codes[:].bitcast(FP8X4), w1_scales[:], tab_words_g[:, jh(h)].bitcast(FP4X4), tab_scales_g[:, jh(h)], start=True, stop=True)
+            nc.scalar.copy(a_sb[:, jh(h)], a_ps[h])
         for h in range(2):
-            nc.scalar.copy(a_sb[:, jh(h)], a_ps[h][:])
-        for h in range(2):
-            nc.vector.tensor_copy(page2[:].indirect(slots(list2, h)), h1[:, jh(h)])
-        nc.vector.tensor_copy(page3[:].indirect(list3[:]), a_sb[:])
+            nc.vector.tensor_tensor(page2[:].indirect(slots(list2, h)), a_sb[:, jh(h)], gain_row[:], ALU.mult)
+            nc.vector.tensor_copy(page3[:].indirect(slots(list3, h)), a_sb[:, jh(h)])
 
         wo_bf = tile("wo_bf", [P, R, PACK], BF16)
         wo_codes = tile("wo_codes", [P, R], U32)
         wo_scales = tile("wo_scales", [P, R], U8)
-        interleave(nc.scalar.copy, wo_bf[:], wo_raw[:])
-        dy_bf = [tile(f"dy_bf{h}", [P, UH, PACK], BF16) for h in range(2)]
+        interleave(nc.vector.tensor_copy, wo_bf[:], wo_raw[:])
+        dy_bf = [tile(f"dy_bf{h}", [P, UH, PACK], BF16, tag=("w1_codes", "w1_scales")[h]) for h in range(2)]
         dy_codes = [tile(f"dy_codes{h}", [P, UH], U32) for h in range(2)]
         dy_scales = [tile(f"dy_scales{h}", [P, UH], U8) for h in range(2)]
         dy_pieces = [dy_raw[0][:, :, :DY_CHUNK], dy_raw[0][:, :, DY_CHUNK:], dy_raw[1][:], dy_raw[2][:]]
         for c in range(U // DY_CHUNK):
             h, part = divmod(c, UH // DY_CHUNK)
             interleave(nc.scalar.copy, dy_bf[h][:, part * DY_CHUNK : (part + 1) * DY_CHUNK, :], dy_pieces[c])
-        gain_row = tile("gain_row", [P, JH], F32)
-        nc.scalar.copy(gain_row[:], gain_col[:].to_broadcast([P, JH]))
-        gain2_col = tile("gain2_col", [P, 1], F32)
-        nc.scalar.mul(gain2_col[:], gain_col[:], 2.0)
 
         x = tile("x", [P, U], F32)
         t = tile("t", [P, U], F32, tag="dy_raw2")
         t2 = tile("t2", [P, U], F32)
         for h in range(2):
-            nc.gpsimd.tensor_tensor(x[:, uh(h)], page2[:, uh(h)], ground_sb[:, uh(h)], ALU.add)
+            nc.vector.tensor_tensor(x[:, uh(h)], page2[:, uh(h)], ground_sb[:, uh(h)], ALU.add)
             nc.scalar.activation(t[:, uh(h)], x[:, uh(h)], ACT.Tanh)
         for h in range(2):
             nc.scalar.activation(t2[:, uh(h)], t[:, uh(h)], ACT.Square)
 
         nc.vector.quantize_mx(wo_codes[:].bitcast(FP8X4), wo_scales[:], wo_bf[:].rearrange("p r j -> p (r j)"))
-        c0 = [ps.tile([P, UH], F32, name=f"c0_{h}") for h in range(2)]
+        c0_banks = ps.tile([P, 2, UH], F32, name="c0_banks", tag="B")
+        c0 = [c0_banks[:, h, :UH] for h in range(2)]
         for h in range(2):
             nc.vector.quantize_mx(dy_codes[h][:].bitcast(FP8X4), dy_scales[h][:], dy_bf[h][:].rearrange("p u j -> p (u j)"))
-            nc.tensor.matmul_mx(c0[h][:], wo_codes[:].bitcast(FP8X4), wo_scales[:], dy_codes[h][:].bitcast(FP8X4), dy_scales[h][:], start=True, stop=True)
+            nc.tensor.matmul_mx(c0[h], wo_codes[:].bitcast(FP8X4), wo_scales[:], dy_codes[h][:].bitcast(FP8X4), dy_scales[h][:], start=True, stop=True)
 
-        b = tile("b", [P, U], F32, tag="dy_bf1")
+        b = tile("b", [P, U], F32, tag="w1_scales")
         dpa = tile("dpa", [P, U], F32)
         dpb = tile("dpb", [P, U], F32)
         ncs = tile("ncs", [P, U], F32)
-        nc.gpsimd.tensor_tensor(b[:, :B_SPLIT], page3[:, :B_SPLIT], ground_sb[:, :B_SPLIT], ALU.add)
-        nc.vector.tensor_tensor(b[:, B_SPLIT:], page3[:, B_SPLIT:], ground_sb[:, B_SPLIT:], ALU.add)
+        nc.gpsimd.tensor_tensor(b[:], page3[:], ground_sb[:], ALU.add)
         for h in range(2):
-            nc.vector.tensor_tensor(dpb[:, uh(h)], c0[h][:], t[:, uh(h)], ALU.mult)
+            nc.vector.tensor_tensor(dpb[:, uh(h)], c0[h], t[:, uh(h)], ALU.mult)
         for h in range(2):
-            nc.vector.scalar_tensor_tensor(ncs[:, uh(h)], t2[:, uh(h)], 1.0, c0[h][:], ALU.subtract, ALU.mult)
+            nc.vector.scalar_tensor_tensor(ncs[:, uh(h)], t2[:, uh(h)], 1.0, c0[h], ALU.subtract, ALU.mult)
         for h in range(2):
             nc.vector.scalar_tensor_tensor(dpa[:, uh(h)], ncs[:, uh(h)], -1.0, b[:, uh(h)], ALU.mult, ALU.mult)
 
+        ncs_turned = tile("ncs_turned", [P, U], F32)
+        ncst_ps_banks = ps.tile([P, 2, UH], F32, name="ncst_ps_banks", tag="C")
+        ncst_ps = [ncst_ps_banks[:, h, :UH] for h in range(2)]
+        ncs_ps_banks = ps.tile([P, 2, UH], F32, name="ncs_ps_banks", tag="D")
+        ncs_ps = [ncs_ps_banks[:, h, :UH] for h in range(2)]
+        for h in range(2):
+            turn_into(ncst_ps[h], ncs[:, uh(h)], True, True)
+            nc.scalar.copy(ncs_turned[:, uh(h)], ncst_ps[h])
+        for h in range(2):
+            turn_into(ncs_ps[h], ncs_turned[:, uh(h)], True, True)
+
         dh1g = tile("dh1g", [P, J], F32)
         da = tile("da", [P, J], F32)
-        hda = tile("hda", [P, J], F32)
-        hdh1 = tile("hdh1", [P, J], F32)
+        e = tile("e", [P, U], F32)
         for h in range(2):
             nc.vector.tensor_tensor(dh1g[:, jh(h)], dpa[:].indirect(slots(list2, h)), gain_row[:], ALU.mult)
         for h in range(2):
             nc.vector.tensor_tensor(da[:, jh(h)], dpb[:].indirect(slots(list3, h)), dh1g[:, jh(h)], ALU.add)
-            nc.scalar.activation(hdh1[:, jh(h)], da[:, jh(h)], ACT.Copy, scale=gain2_col[:])
-        nc.scalar.mul(hda[:], da[:], 2.0)
         for h in range(2):
-            nc.vector.tensor_copy(page2[:].indirect(slots(list2, h)), hdh1[:, jh(h)])
-        nc.vector.tensor_copy(page3[:].indirect(list3[:]), hda[:])
+            nc.vector.scalar_tensor_tensor(e[:, uh(h)], t[:, uh(h)], -2.0, dpa[:, uh(h)], ALU.mult, ALU.mult)
+        for h in range(2):
+            nc.vector.tensor_tensor(page3[:].indirect(slots(list3, h)), da[:, jh(h)], da[:, jh(h)], ALU.add)
+            nc.vector.tensor_tensor(page2[:].indirect(slots(list2, h)), da[:, jh(h)], gain2_row[:], ALU.mult)
 
-        cs = tile("cs", [P, U], F32)
-        tm2 = tile("tm2", [P, U], F32)
-        e = tile("e", [P, U], F32, tag="dpb")
-        nc.scalar.mul(tm2[:], t[:], -2.0)
-        nc.scalar.mul(cs[:], ncs[:], -1.0)
-        nc.gpsimd.tensor_tensor(e[:], tm2[:], dpa[:], ALU.mult)
         hpa = tile("hpa", [P, U], F32)
         hpb = tile("hpb", [P, U], F32)
         m1 = tile("m1", [P, U], F32)
-        m2 = tile("m2", [P, U], F32)
+        nm2 = tile("nm2", [P, U], F32)
         nc.gpsimd.tensor_tensor(m1[:], page2[:], e[:], ALU.mult)
-        nc.gpsimd.tensor_tensor(hpb[:, :HPB_SPLIT], page2[:, :HPB_SPLIT], cs[:, :HPB_SPLIT], ALU.mult)
         for h in range(2):
-            nc.vector.tensor_tensor(m2[:, uh(h)], page3[:, uh(h)], cs[:, uh(h)], ALU.mult)
-        nc.vector.tensor_tensor(hpb[:, HPB_SPLIT:], page2[:, HPB_SPLIT:], cs[:, HPB_SPLIT:], ALU.mult)
+            nc.vector.tensor_tensor(nm2[:, uh(h)], ncs_ps[h], page3[:, uh(h)], ALU.mult)
         for h in range(2):
-            nc.vector.tensor_tensor(hpa[:, uh(h)], m1[:, uh(h)], m2[:, uh(h)], ALU.add)
+            nc.vector.scalar_tensor_tensor(hpb[:, uh(h)], page2[:, uh(h)], -1.0, ncs_ps[h], ALU.mult, ALU.mult)
+        for h in range(2):
+            nc.vector.tensor_tensor(hpa[:, uh(h)], m1[:, uh(h)], nm2[:, uh(h)], ALU.subtract)
 
         hh1g = tile("hh1g", [P, J], F32)
         ha = tile("ha", [P, J], F32)

@@ -19,14 +19,30 @@ ACT = mybir.ActivationFunctionType
 
 P = 128
 PACK = 4
+GROUP = 16
+QUADRANT = 32
+LINE = 4
+BANK = 512
 JH = J // 2
 UH = U // 2
-DY_CHUNK = 256
+DY_CAST = 256
 DY_LOADS = (512, 256, 256)
 
 
 def interleave(copy, grouped, raw):
-    copy(grouped.rearrange("p (c i) t -> p c t i", i=4), raw.rearrange("p t (c i) -> p c t i", i=4))
+    copy(grouped.rearrange("p (c i) t -> p c t i", i=LINE), raw.rearrange("p t (c i) -> p c t i", i=LINE))
+
+
+def slots(offsets, h):
+    return offsets[:, h * (JH // GROUP) : (h + 1) * (JH // GROUP)]
+
+
+def jh(h):
+    return slice(h * JH, (h + 1) * JH)
+
+
+def uh(h):
+    return slice(h * UH, (h + 1) * UH)
 
 
 def tile_attend_gptwopages_kernel(tc, tab_words, tab_scales, w1, gain, ground, wo, dy, og, base, offs, offs2, offs3, out):
@@ -35,105 +51,106 @@ def tile_attend_gptwopages_kernel(tc, tab_words, tab_scales, w1, gain, ground, w
         sb = ctx.enter_context(tc.tile_pool(name="sb", bufs=1))
         ps = ctx.enter_context(tc.psum_pool(name="ps", bufs=1))
 
-        def tile(name, shape, dtype, tag=None):
-            return sb.tile(shape, dtype, name=name, tag=tag or name, align_bytes=64)
+        def tile(name, shape, dtype, reuses=None):
+            return sb.tile(shape, dtype, name=name, tag=reuses or name, align_bytes=64)
 
-        list1 = tile("list1", [P, J // 16], U16)
-        list2 = tile("list2", [P, J // 16], U16)
-        list3 = tile("list3", [P, J // 16], U16)
+        def two_banks(name, width):
+            banks = ps.tile([P, 2, BANK], F32, name=name)
+            return [banks[:, h, :width] for h in range(2)]
+
+        list1 = tile("list1", [P, J // GROUP], U16)
+        list2 = tile("list2", [P, J // GROUP], U16)
+        list3 = tile("list3", [P, J // GROUP], U16)
         words = tile("words", [P, T], U16)
         scales = tile("scales", [P, T], U8)
         w1_raw = tile("w1_raw", [P, PACK, R], F32)
         wo_raw = tile("wo_raw", [P, PACK, R], F32)
-        dy_raw = [tile(f"dy_raw{c}", [P, PACK, w], F32) for c, w in enumerate(DY_LOADS)]
+        dy_raw = [tile(f"dy_raw{c}", [P, PACK, width], F32) for c, width in enumerate(DY_LOADS)]
         gain_col = tile("gain_col", [P, 1], F32)
         og_col = tile("og_col", [P, 1], F32)
         ground_sb = tile("ground_sb", [P, U], F32)
         base_sb = tile("base_sb", [P, J], F32)
         page2 = tile("page2", [P, U], F32)
         page3 = tile("page3", [P, U], F32)
-        warm = tile("warm", [P, 8], F32)
 
         nc.vector.memset(scales[:, : T // 2].bitcast(I32), 0)
         nc.gpsimd.memset(scales[:, T // 2 :].bitcast(I32), 0)
-        nc.vector.memset(warm[:], 0.0)
-        nc.scalar.activation(warm[:], warm[:], ACT.Tanh)
         nc.vector.memset(page2[:], 0.0)
         nc.vector.memset(page3[:], 0.0)
 
         nc.sync.dma_start(list1[:], offs)
-        nc.sync.dma_start(w1_raw[:], w1.rearrange("(p j) r -> p j r", j=PACK))
-        for q in range(4):
-            nc.sync.dma_start(scales[32 * q : 32 * q + 4, :].bitcast(I32), tab_scales[0, 4 * q : 4 * q + 4, :].bitcast(I32))
+        nc.sync.dma_start(w1_raw[:], w1.rearrange("(p t) r -> p t r", t=PACK))
+        for q in range(P // QUADRANT):
+            nc.sync.dma_start(
+                scales[QUADRANT * q : QUADRANT * q + 4, :].bitcast(I32),
+                tab_scales[0, 4 * q : 4 * q + 4, :].bitcast(I32),
+            )
         nc.sync.dma_start(words[:].bitcast(I32), tab_words[0].bitcast(I32))
         nc.gpsimd.dma_start(gain_col[:], gain)
         nc.sync.dma_start(list2[:], offs2)
-        nc.sync.dma_start(wo_raw[:], wo.rearrange("(p j) r -> p j r", j=PACK))
+        nc.sync.dma_start(wo_raw[:], wo.rearrange("(p t) r -> p t r", t=PACK))
         nc.sync.dma_start(list3[:], offs3)
-        dy_view = dy.rearrange("(p j) u -> p j u", j=PACK)
-        nc.sync.dma_start(dy_raw[0][:], dy_view[:, :, 0:512])
-        nc.sync.dma_start(ground_sb[:], ground)
-        nc.sync.dma_start(dy_raw[1][:], dy_view[:, :, 512:768])
-        nc.sync.dma_start(dy_raw[2][:], dy_view[:, :, 768:1024])
+        dy_view = dy.rearrange("(p t) u -> p t u", t=PACK)
+        for c, width in enumerate(DY_LOADS):
+            first = sum(DY_LOADS[:c])
+            nc.sync.dma_start(dy_raw[c][:], dy_view[:, :, first : first + width])
+            if c == 0:
+                nc.sync.dma_start(ground_sb[:], ground)
         nc.sync.dma_start(og_col[:], og)
         nc.sync.dma_start(base_sb[:], base)
-
-        def slots(lst, h):
-            return lst[:, h * (JH // 16) : (h + 1) * (JH // 16)]
-
-        def jh(h):
-            return slice(h * JH, (h + 1) * JH)
-
-        def uh(h):
-            return slice(h * UH, (h + 1) * UH)
 
         ident = tile("ident", [P, P], F32)
         make_identity(nc, ident[:])
 
-        def turn_into(bank, src, first, last):
+        def transpose_blocks(bank, src):
             blocks = src.shape[1] // P
             for j in range(blocks):
                 cols = slice(j * P, (j + 1) * P)
-                nc.tensor.matmul(bank[:, cols], src[:, cols], ident[:], start=first and j == 0, stop=last and j == blocks - 1, is_transpose=True)
+                nc.tensor.matmul(bank[:, cols], src[:, cols], ident[:], start=j == 0, stop=j == blocks - 1, is_transpose=True)
 
         gain_row = tile("gain_row", [P, JH], F32)
-        gain2_row = tile("gain2_row", [P, JH], F32)
         nc.scalar.copy(gain_row[:], gain_col[:].to_broadcast([P, JH]))
-        nc.scalar.mul(gain2_row[:], gain_row[:], 2.0)
 
         w1_bf = tile("w1_bf", [P, R, PACK], BF16)
         w1_codes = tile("w1_codes", [P, R], U32)
         w1_scales = tile("w1_scales", [P, R], U8)
         interleave(nc.vector.tensor_copy, w1_bf[:], w1_raw[:])
-        tab_scales_g = tile("tab_scales_g", [P, J], U8)
-        tab_words_g = tile("tab_words_g", [P, J], U16)
-        nc.vector.quantize_mx(w1_codes[:].bitcast(FP8X4), w1_scales[:], w1_bf[:].rearrange("p r j -> p (r j)"))
-        a_sb = tile("a_sb", [P, J], F32)
-        a_banks = ps.tile([P, 2, UH], F32, name="a_banks", tag="A")
-        a_ps = [a_banks[:, h, :JH] for h in range(2)]
+        listed_scales = tile("listed_scales", [P, J], U8)
+        listed_words = tile("listed_words", [P, J], U16)
+        nc.vector.quantize_mx(w1_codes[:].bitcast(FP8X4), w1_scales[:], w1_bf[:].rearrange("p r t -> p (r t)"))
+        a = tile("a", [P, J], F32)
+        a_ps = two_banks("a_ps", JH)
         for h in range(2):
-            nc.vector.tensor_copy(tab_scales_g[:, jh(h)], scales[:].indirect(slots(list1, h)))
-            nc.vector.tensor_copy(tab_words_g[:, jh(h)], words[:].indirect(slots(list1, h)))
-            nc.tensor.matmul_mx(a_ps[h], w1_codes[:].bitcast(FP8X4), w1_scales[:], tab_words_g[:, jh(h)].bitcast(FP4X4), tab_scales_g[:, jh(h)], start=True, stop=True)
-            nc.scalar.copy(a_sb[:, jh(h)], a_ps[h])
+            nc.vector.tensor_copy(listed_scales[:, jh(h)], scales[:].indirect(slots(list1, h)))
+            nc.vector.tensor_copy(listed_words[:, jh(h)], words[:].indirect(slots(list1, h)))
+            nc.tensor.matmul_mx(
+                a_ps[h],
+                w1_codes[:].bitcast(FP8X4),
+                w1_scales[:],
+                listed_words[:, jh(h)].bitcast(FP4X4),
+                listed_scales[:, jh(h)],
+                start=True,
+                stop=True,
+            )
+            nc.scalar.copy(a[:, jh(h)], a_ps[h])
         for h in range(2):
-            nc.vector.tensor_tensor(page2[:].indirect(slots(list2, h)), a_sb[:, jh(h)], gain_row[:], ALU.mult)
-            nc.vector.tensor_copy(page3[:].indirect(slots(list3, h)), a_sb[:, jh(h)])
+            nc.vector.tensor_tensor(page2[:].indirect(slots(list2, h)), a[:, jh(h)], gain_row[:], ALU.mult)
+            nc.vector.tensor_copy(page3[:].indirect(slots(list3, h)), a[:, jh(h)])
 
         wo_bf = tile("wo_bf", [P, R, PACK], BF16)
         wo_codes = tile("wo_codes", [P, R], U32)
         wo_scales = tile("wo_scales", [P, R], U8)
-        interleave(nc.vector.tensor_copy, wo_bf[:], wo_raw[:])
-        dy_bf = [tile(f"dy_bf{h}", [P, UH, PACK], BF16, tag=("w1_codes", "w1_scales")[h]) for h in range(2)]
+        interleave(nc.scalar.copy, wo_bf[:], wo_raw[:])
+        dy_bf = [tile(f"dy_bf{h}", [P, UH, PACK], BF16, reuses=("w1_codes", "w1_scales")[h]) for h in range(2)]
         dy_codes = [tile(f"dy_codes{h}", [P, UH], U32) for h in range(2)]
         dy_scales = [tile(f"dy_scales{h}", [P, UH], U8) for h in range(2)]
-        dy_pieces = [dy_raw[0][:, :, :DY_CHUNK], dy_raw[0][:, :, DY_CHUNK:], dy_raw[1][:], dy_raw[2][:]]
-        for c in range(U // DY_CHUNK):
-            h, part = divmod(c, UH // DY_CHUNK)
-            interleave(nc.scalar.copy, dy_bf[h][:, part * DY_CHUNK : (part + 1) * DY_CHUNK, :], dy_pieces[c])
+        dy_pieces = [raw[:, :, c : c + DY_CAST] for raw, width in zip(dy_raw, DY_LOADS) for c in range(0, width, DY_CAST)]
+        for c, piece in enumerate(dy_pieces):
+            h, part = divmod(c, UH // DY_CAST)
+            interleave(nc.scalar.copy, dy_bf[h][:, part * DY_CAST : (part + 1) * DY_CAST, :], piece)
 
         x = tile("x", [P, U], F32)
-        t = tile("t", [P, U], F32, tag="dy_raw2")
+        t = tile("t", [P, U], F32, reuses=f"dy_raw{len(DY_LOADS) - 1}")
         t2 = tile("t2", [P, U], F32)
         for h in range(2):
             nc.vector.tensor_tensor(x[:, uh(h)], page2[:, uh(h)], ground_sb[:, uh(h)], ALU.add)
@@ -141,14 +158,21 @@ def tile_attend_gptwopages_kernel(tc, tab_words, tab_scales, w1, gain, ground, w
         for h in range(2):
             nc.scalar.activation(t2[:, uh(h)], t[:, uh(h)], ACT.Square)
 
-        nc.vector.quantize_mx(wo_codes[:].bitcast(FP8X4), wo_scales[:], wo_bf[:].rearrange("p r j -> p (r j)"))
-        c0_banks = ps.tile([P, 2, UH], F32, name="c0_banks", tag="B")
-        c0 = [c0_banks[:, h, :UH] for h in range(2)]
+        nc.vector.quantize_mx(wo_codes[:].bitcast(FP8X4), wo_scales[:], wo_bf[:].rearrange("p r t -> p (r t)"))
+        c0 = two_banks("c0", UH)
         for h in range(2):
-            nc.vector.quantize_mx(dy_codes[h][:].bitcast(FP8X4), dy_scales[h][:], dy_bf[h][:].rearrange("p u j -> p (u j)"))
-            nc.tensor.matmul_mx(c0[h], wo_codes[:].bitcast(FP8X4), wo_scales[:], dy_codes[h][:].bitcast(FP8X4), dy_scales[h][:], start=True, stop=True)
+            nc.vector.quantize_mx(dy_codes[h][:].bitcast(FP8X4), dy_scales[h][:], dy_bf[h][:].rearrange("p u t -> p (u t)"))
+            nc.tensor.matmul_mx(
+                c0[h],
+                wo_codes[:].bitcast(FP8X4),
+                wo_scales[:],
+                dy_codes[h][:].bitcast(FP8X4),
+                dy_scales[h][:],
+                start=True,
+                stop=True,
+            )
 
-        b = tile("b", [P, U], F32, tag="w1_scales")
+        b = tile("b", [P, U], F32, reuses="w1_scales")
         dpa = tile("dpa", [P, U], F32)
         dpb = tile("dpb", [P, U], F32)
         ncs = tile("ncs", [P, U], F32)
@@ -161,23 +185,23 @@ def tile_attend_gptwopages_kernel(tc, tab_words, tab_scales, w1, gain, ground, w
             nc.vector.scalar_tensor_tensor(dpa[:, uh(h)], ncs[:, uh(h)], -1.0, b[:, uh(h)], ALU.mult, ALU.mult)
 
         ncs_turned = tile("ncs_turned", [P, U], F32)
-        ncst_ps_banks = ps.tile([P, 2, UH], F32, name="ncst_ps_banks", tag="C")
-        ncst_ps = [ncst_ps_banks[:, h, :UH] for h in range(2)]
-        ncs_ps_banks = ps.tile([P, 2, UH], F32, name="ncs_ps_banks", tag="D")
-        ncs_ps = [ncs_ps_banks[:, h, :UH] for h in range(2)]
+        ncs_turned_ps = two_banks("ncs_turned_ps", UH)
+        ncs_ps = two_banks("ncs_ps", UH)
         for h in range(2):
-            turn_into(ncst_ps[h], ncs[:, uh(h)], True, True)
-            nc.scalar.copy(ncs_turned[:, uh(h)], ncst_ps[h])
+            transpose_blocks(ncs_turned_ps[h], ncs[:, uh(h)])
+            nc.scalar.copy(ncs_turned[:, uh(h)], ncs_turned_ps[h])
         for h in range(2):
-            turn_into(ncs_ps[h], ncs_turned[:, uh(h)], True, True)
+            transpose_blocks(ncs_ps[h], ncs_turned[:, uh(h)])
 
-        dh1g = tile("dh1g", [P, J], F32)
+        gain2_row = tile("gain2_row", [P, JH], F32, reuses="x")
+        nc.scalar.mul(gain2_row[:], gain_row[:], 2.0)
+        dh1_gain = tile("dh1_gain", [P, J], F32)
         da = tile("da", [P, J], F32)
         e = tile("e", [P, U], F32)
         for h in range(2):
-            nc.vector.tensor_tensor(dh1g[:, jh(h)], dpa[:].indirect(slots(list2, h)), gain_row[:], ALU.mult)
+            nc.vector.tensor_tensor(dh1_gain[:, jh(h)], dpa[:].indirect(slots(list2, h)), gain_row[:], ALU.mult)
         for h in range(2):
-            nc.vector.tensor_tensor(da[:, jh(h)], dpb[:].indirect(slots(list3, h)), dh1g[:, jh(h)], ALU.add)
+            nc.vector.tensor_tensor(da[:, jh(h)], dpb[:].indirect(slots(list3, h)), dh1_gain[:, jh(h)], ALU.add)
         for h in range(2):
             nc.vector.scalar_tensor_tensor(e[:, uh(h)], t[:, uh(h)], -2.0, dpa[:, uh(h)], ALU.mult, ALU.mult)
         for h in range(2):
@@ -186,23 +210,22 @@ def tile_attend_gptwopages_kernel(tc, tab_words, tab_scales, w1, gain, ground, w
 
         hpa = tile("hpa", [P, U], F32)
         hpb = tile("hpb", [P, U], F32)
-        m1 = tile("m1", [P, U], F32)
-        nm2 = tile("nm2", [P, U], F32)
-        nc.gpsimd.tensor_tensor(m1[:], page2[:], e[:], ALU.mult)
+        s51_e = tile("s51_e", [P, U], F32)
+        s52_ncs = tile("s52_ncs", [P, U], F32)
+        nc.gpsimd.tensor_tensor(s51_e[:], page2[:], e[:], ALU.mult)
         for h in range(2):
-            nc.vector.tensor_tensor(nm2[:, uh(h)], ncs_ps[h], page3[:, uh(h)], ALU.mult)
+            nc.vector.tensor_tensor(s52_ncs[:, uh(h)], ncs_ps[h], page3[:, uh(h)], ALU.mult)
         for h in range(2):
             nc.vector.scalar_tensor_tensor(hpb[:, uh(h)], page2[:, uh(h)], -1.0, ncs_ps[h], ALU.mult, ALU.mult)
-        for h in range(2):
-            nc.vector.tensor_tensor(hpa[:, uh(h)], m1[:, uh(h)], nm2[:, uh(h)], ALU.subtract)
+        nc.vector.tensor_tensor(hpa[:], s51_e[:], s52_ncs[:], ALU.subtract)
 
-        hh1g = tile("hh1g", [P, J], F32)
+        hh1_gain = tile("hh1_gain", [P, J], F32)
         ha = tile("ha", [P, J], F32)
         y = tile("y", [P, J], F32)
         for h in range(2):
-            nc.vector.tensor_tensor(hh1g[:, jh(h)], hpa[:].indirect(slots(list2, h)), gain_row[:], ALU.mult)
+            nc.vector.tensor_tensor(hh1_gain[:, jh(h)], hpa[:].indirect(slots(list2, h)), gain_row[:], ALU.mult)
         for h in range(2):
-            nc.vector.tensor_tensor(ha[:, jh(h)], hpb[:].indirect(slots(list3, h)), hh1g[:, jh(h)], ALU.add)
-        for h in range(2):
-            nc.vector.scalar_tensor_tensor(y[:, jh(h)], ha[:, jh(h)], og_col[:], base_sb[:, jh(h)], ALU.mult, ALU.add)
-            nc.sync.dma_start(out[:, jh(h)], y[:, jh(h)])
+            nc.vector.tensor_tensor(ha[:, jh(h)], hpb[:].indirect(slots(list3, h)), hh1_gain[:, jh(h)], ALU.add)
+        for cols in (slice(0, JH), slice(JH, J - J // 4), slice(J - J // 4, J)):
+            nc.vector.scalar_tensor_tensor(y[:, cols], ha[:, cols], og_col[:], base_sb[:, cols], ALU.mult, ALU.add)
+            nc.sync.dma_start(out[:, cols], y[:, cols])

from contextlib import ExitStack

import concourse.mybir as mybir
from concourse.masks import make_identity

K, R, F, T, J, U = 512, 128, 512, 2048, 512, 1024
FLOPS = 2 * K * R * J + 2 * F * R * U

F32 = mybir.dt.float32
BF16 = mybir.dt.bfloat16
I32 = mybir.dt.int32
U32 = mybir.dt.uint32
U16 = mybir.dt.uint16
U8 = mybir.dt.uint8
FP8X4 = mybir.dt.float8_e4m3fn_x4
FP4X4 = mybir.dt.float4_e2m1fn_x4
ALU = mybir.AluOpType
ACT = mybir.ActivationFunctionType

P = 128
PACK = 4
GROUP = 16
QUADRANT = 32
LINE = 4
BANK = 512
JH = J // 2
UH = U // 2
DY_CAST = 256
DY_LOADS = (512, 256, 256)


def interleave(copy, grouped, raw):
    copy(grouped.rearrange("p (c i) t -> p c t i", i=LINE), raw.rearrange("p t (c i) -> p c t i", i=LINE))


def slots(offsets, h):
    return offsets[:, h * (JH // GROUP) : (h + 1) * (JH // GROUP)]


def jh(h):
    return slice(h * JH, (h + 1) * JH)


def uh(h):
    return slice(h * UH, (h + 1) * UH)


def tile_attend_gptwopages_kernel(tc, tab_words, tab_scales, w1, gain, ground, wo, dy, og, base, offs, offs2, offs3, out):
    nc = tc.nc
    with ExitStack() as ctx:
        sb = ctx.enter_context(tc.tile_pool(name="sb", bufs=1))
        ps = ctx.enter_context(tc.psum_pool(name="ps", bufs=1))

        def tile(name, shape, dtype, reuses=None):
            return sb.tile(shape, dtype, name=name, tag=reuses or name, align_bytes=64)

        def two_banks(name, width):
            banks = ps.tile([P, 2, BANK], F32, name=name)
            return [banks[:, h, :width] for h in range(2)]

        list1 = tile("list1", [P, J // GROUP], U16)
        list2 = tile("list2", [P, J // GROUP], U16)
        list3 = tile("list3", [P, J // GROUP], U16)
        words = tile("words", [P, T], U16)
        scales = tile("scales", [P, T], U8)
        w1_raw = tile("w1_raw", [P, PACK, R], F32)
        wo_raw = tile("wo_raw", [P, PACK, R], F32)
        dy_raw = [tile(f"dy_raw{c}", [P, PACK, width], F32) for c, width in enumerate(DY_LOADS)]
        gain_col = tile("gain_col", [P, 1], F32)
        og_col = tile("og_col", [P, 1], F32)
        ground_sb = tile("ground_sb", [P, U], F32)
        base_sb = tile("base_sb", [P, J], F32)
        page2 = tile("page2", [P, U], F32)
        page3 = tile("page3", [P, U], F32)

        nc.vector.memset(scales[:, : T // 2].bitcast(I32), 0)
        nc.gpsimd.memset(scales[:, T // 2 :].bitcast(I32), 0)
        nc.vector.memset(page2[:], 0.0)
        nc.vector.memset(page3[:], 0.0)

        nc.sync.dma_start(list1[:], offs)
        nc.sync.dma_start(w1_raw[:], w1.rearrange("(p t) r -> p t r", t=PACK))
        for q in range(P // QUADRANT):
            nc.sync.dma_start(
                scales[QUADRANT * q : QUADRANT * q + 4, :].bitcast(I32),
                tab_scales[0, 4 * q : 4 * q + 4, :].bitcast(I32),
            )
        nc.sync.dma_start(words[:].bitcast(I32), tab_words[0].bitcast(I32))
        nc.gpsimd.dma_start(gain_col[:], gain)
        nc.sync.dma_start(list2[:], offs2)
        nc.sync.dma_start(wo_raw[:], wo.rearrange("(p t) r -> p t r", t=PACK))
        nc.sync.dma_start(list3[:], offs3)
        dy_view = dy.rearrange("(p t) u -> p t u", t=PACK)
        for c, width in enumerate(DY_LOADS):
            first = sum(DY_LOADS[:c])
            nc.sync.dma_start(dy_raw[c][:], dy_view[:, :, first : first + width])
            if c == 0:
                nc.sync.dma_start(ground_sb[:], ground)
        nc.sync.dma_start(og_col[:], og)
        nc.sync.dma_start(base_sb[:], base)

        ident = tile("ident", [P, P], F32)
        make_identity(nc, ident[:])

        def transpose_blocks(bank, src):
            blocks = src.shape[1] // P
            for j in range(blocks):
                cols = slice(j * P, (j + 1) * P)
                nc.tensor.matmul(bank[:, cols], src[:, cols], ident[:], start=j == 0, stop=j == blocks - 1, is_transpose=True)

        gain_row = tile("gain_row", [P, JH], F32)
        nc.scalar.copy(gain_row[:], gain_col[:].to_broadcast([P, JH]))

        w1_bf = tile("w1_bf", [P, R, PACK], BF16)
        w1_codes = tile("w1_codes", [P, R], U32)
        w1_scales = tile("w1_scales", [P, R], U8)
        interleave(nc.vector.tensor_copy, w1_bf[:], w1_raw[:])
        listed_scales = tile("listed_scales", [P, J], U8)
        listed_words = tile("listed_words", [P, J], U16)
        nc.vector.quantize_mx(w1_codes[:].bitcast(FP8X4), w1_scales[:], w1_bf[:].rearrange("p r t -> p (r t)"))
        a = tile("a", [P, J], F32)
        a_ps = two_banks("a_ps", JH)
        for h in range(2):
            nc.vector.tensor_copy(listed_scales[:, jh(h)], scales[:].indirect(slots(list1, h)))
            nc.vector.tensor_copy(listed_words[:, jh(h)], words[:].indirect(slots(list1, h)))
            nc.tensor.matmul_mx(
                a_ps[h],
                w1_codes[:].bitcast(FP8X4),
                w1_scales[:],
                listed_words[:, jh(h)].bitcast(FP4X4),
                listed_scales[:, jh(h)],
                start=True,
                stop=True,
            )
            nc.scalar.copy(a[:, jh(h)], a_ps[h])
        for h in range(2):
            nc.vector.tensor_tensor(page2[:].indirect(slots(list2, h)), a[:, jh(h)], gain_row[:], ALU.mult)
            nc.vector.tensor_copy(page3[:].indirect(slots(list3, h)), a[:, jh(h)])

        wo_bf = tile("wo_bf", [P, R, PACK], BF16)
        wo_codes = tile("wo_codes", [P, R], U32)
        wo_scales = tile("wo_scales", [P, R], U8)
        interleave(nc.scalar.copy, wo_bf[:], wo_raw[:])
        dy_bf = [tile(f"dy_bf{h}", [P, UH, PACK], BF16, reuses=("w1_codes", "w1_scales")[h]) for h in range(2)]
        dy_codes = [tile(f"dy_codes{h}", [P, UH], U32) for h in range(2)]
        dy_scales = [tile(f"dy_scales{h}", [P, UH], U8) for h in range(2)]
        dy_pieces = [raw[:, :, c : c + DY_CAST] for raw, width in zip(dy_raw, DY_LOADS) for c in range(0, width, DY_CAST)]
        for c, piece in enumerate(dy_pieces):
            h, part = divmod(c, UH // DY_CAST)
            interleave(nc.scalar.copy, dy_bf[h][:, part * DY_CAST : (part + 1) * DY_CAST, :], piece)

        x = tile("x", [P, U], F32)
        t = tile("t", [P, U], F32, reuses=f"dy_raw{len(DY_LOADS) - 1}")
        t2 = tile("t2", [P, U], F32)
        for h in range(2):
            nc.vector.tensor_tensor(x[:, uh(h)], page2[:, uh(h)], ground_sb[:, uh(h)], ALU.add)
            nc.scalar.activation(t[:, uh(h)], x[:, uh(h)], ACT.Tanh)
        for h in range(2):
            nc.scalar.activation(t2[:, uh(h)], t[:, uh(h)], ACT.Square)

        nc.vector.quantize_mx(wo_codes[:].bitcast(FP8X4), wo_scales[:], wo_bf[:].rearrange("p r t -> p (r t)"))
        c0 = two_banks("c0", UH)
        for h in range(2):
            nc.vector.quantize_mx(dy_codes[h][:].bitcast(FP8X4), dy_scales[h][:], dy_bf[h][:].rearrange("p u t -> p (u t)"))
            nc.tensor.matmul_mx(
                c0[h],
                wo_codes[:].bitcast(FP8X4),
                wo_scales[:],
                dy_codes[h][:].bitcast(FP8X4),
                dy_scales[h][:],
                start=True,
                stop=True,
            )

        b = tile("b", [P, U], F32, reuses="w1_scales")
        dpa = tile("dpa", [P, U], F32)
        dpb = tile("dpb", [P, U], F32)
        ncs = tile("ncs", [P, U], F32)
        nc.gpsimd.tensor_tensor(b[:], page3[:], ground_sb[:], ALU.add)
        for h in range(2):
            nc.vector.tensor_tensor(dpb[:, uh(h)], c0[h], t[:, uh(h)], ALU.mult)
        for h in range(2):
            nc.vector.scalar_tensor_tensor(ncs[:, uh(h)], t2[:, uh(h)], 1.0, c0[h], ALU.subtract, ALU.mult)
        for h in range(2):
            nc.vector.scalar_tensor_tensor(dpa[:, uh(h)], ncs[:, uh(h)], -1.0, b[:, uh(h)], ALU.mult, ALU.mult)

        ncs_turned = tile("ncs_turned", [P, U], F32)
        ncs_turned_ps = two_banks("ncs_turned_ps", UH)
        ncs_ps = two_banks("ncs_ps", UH)
        for h in range(2):
            transpose_blocks(ncs_turned_ps[h], ncs[:, uh(h)])
            nc.scalar.copy(ncs_turned[:, uh(h)], ncs_turned_ps[h])
        for h in range(2):
            transpose_blocks(ncs_ps[h], ncs_turned[:, uh(h)])

        gain2_row = tile("gain2_row", [P, JH], F32, reuses="x")
        nc.scalar.mul(gain2_row[:], gain_row[:], 2.0)
        dh1_gain = tile("dh1_gain", [P, J], F32)
        da = tile("da", [P, J], F32)
        e = tile("e", [P, U], F32)
        for h in range(2):
            nc.vector.tensor_tensor(dh1_gain[:, jh(h)], dpa[:].indirect(slots(list2, h)), gain_row[:], ALU.mult)
        for h in range(2):
            nc.vector.tensor_tensor(da[:, jh(h)], dpb[:].indirect(slots(list3, h)), dh1_gain[:, jh(h)], ALU.add)
        for h in range(2):
            nc.vector.scalar_tensor_tensor(e[:, uh(h)], t[:, uh(h)], -2.0, dpa[:, uh(h)], ALU.mult, ALU.mult)
        for h in range(2):
            nc.vector.tensor_tensor(page3[:].indirect(slots(list3, h)), da[:, jh(h)], da[:, jh(h)], ALU.add)
            nc.vector.tensor_tensor(page2[:].indirect(slots(list2, h)), da[:, jh(h)], gain2_row[:], ALU.mult)

        hpa = tile("hpa", [P, U], F32)
        hpb = tile("hpb", [P, U], F32)
        s51_e = tile("s51_e", [P, U], F32)
        s52_ncs = tile("s52_ncs", [P, U], F32)
        nc.gpsimd.tensor_tensor(s51_e[:], page2[:], e[:], ALU.mult)
        for h in range(2):
            nc.vector.tensor_tensor(s52_ncs[:, uh(h)], ncs_ps[h], page3[:, uh(h)], ALU.mult)
        for h in range(2):
            nc.vector.scalar_tensor_tensor(hpb[:, uh(h)], page2[:, uh(h)], -1.0, ncs_ps[h], ALU.mult, ALU.mult)
        nc.vector.tensor_tensor(hpa[:], s51_e[:], s52_ncs[:], ALU.subtract)

        hh1_gain = tile("hh1_gain", [P, J], F32)
        ha = tile("ha", [P, J], F32)
        y = tile("y", [P, J], F32)
        for h in range(2):
            nc.vector.tensor_tensor(hh1_gain[:, jh(h)], hpa[:].indirect(slots(list2, h)), gain_row[:], ALU.mult)
        for h in range(2):
            nc.vector.tensor_tensor(ha[:, jh(h)], hpb[:].indirect(slots(list3, h)), hh1_gain[:, jh(h)], ALU.add)
        for cols in (slice(0, JH), slice(JH, J - J // 4), slice(J - J // 4, J)):
            nc.vector.scalar_tensor_tensor(y[:, cols], ha[:, cols], og_col[:], base_sb[:, cols], ALU.mult, ALU.add)
            nc.sync.dma_start(out[:, cols], y[:, cols])
